import numpy as np
CORES = [15,47,79,175,207]
N = 5
C = 512
def setup_inputs(rng):
    return {"x": rng.standard_normal((N, 128, C), dtype=np.float32)}
def setup_inputs_big(rng):
    d = setup_inputs(rng)
    for k in ("x",): d[k] = (d[k].astype(np.float32) * 1048576.0).astype(d[k].dtype)
    return d
def setup_inputs_small(rng):
    d = setup_inputs(rng)
    for k in ("x",): d[k] = (d[k].astype(np.float32) * (1 / 1048576.0)).astype(d[k].dtype)
    return d
def setup_inputs_apart(rng):
    d = setup_inputs(rng)
    f = (10.0 ** rng.permutation(np.linspace(-1.5, 1.5, N))).astype(np.float32).reshape(N, 1, 1)
    for k in ("x",): d[k] = (d[k].astype(np.float32) * f).astype(d[k].dtype)
    return d
def reference(x):
    X = x.astype(np.float64)
    y = np.stack([sum(np.maximum(X[r] - X[s], 0.0) for s in range(N)) for r in range(N)])
    return {"y": y.astype(np.float32)}

@@ -1,0 +1,149 @@
+from concourse.bass import DstId, RemoteDMATransfer
+from concourse.mybir import AluOpType
+
+N = 5
+C = 512
+WORLD = 256
+NH = 0
+NH_OWN = 0
+CH = 0
+CD = C - NH * CH
+ORDER = [(0, 1), (0, 2), (0, 3), (0, 4)] if NH == 0 else [(0, 1), (0, 2), (0, 3), (1, 1), (1, 2), (1, 3), (0, 4), (1, 4)]
+LAST_SPLIT = 2 if NH == 0 else 1
+
+SCRATCH = {
+    "xs": ("sbuf", [128, C], "float32"),
+    "land": ("sbuf", [128, (N - 1) * C], "float32"),
+    "acc": ("sbuf", [128, C], "float32"),
+    "xp": ("psum", [128, C], "float32"),
+    "q": ("psum", [128, C], "float32"),
+    "t": ("psum", [128, C], "float32"),
+}
+SEMAPHORES = (["ld0", "ld1", "fed", "sent", "vs"] + ["a0_%d" % k for k in range(1, N)] + ["a1_%d" % k for k in range(1, N)]
+              + ["st%d" % i for i in range(4)])
+
+
+def _bits(mask):
+    return [b for b in range(32) if (mask >> b) & 1]
+
+
+def _count(mask):
+    return len(_bits(mask))
+
+
+def _helpers(rc, T, topo):
+    peers = [d for d in T.cores if d != rc]
+    cand = [c for c in range(WORLD)
+            if topo.host(c) == topo.host(rc) and topo.chip(c) == topo.chip(rc) and T.rank_of(c) is None
+            and all(topo.may_write(c, d) for d in peers)]
+    own = [c for c in cand if topo.die(c) == topo.die(rc)]
+    far = [c for c in cand if topo.die(c) != topo.die(rc)]
+    return far[:NH - NH_OWN] + own[:NH_OWN]
+
+
+def _block(j):
+    return CD + j * CH, CD + (j + 1) * CH
+
+
+def _send_round(g, core, rank, T, topo, a, b, region):
+    total = 0
+    for k in range(1, N):
+        d = T.cores[(rank + k) % N]
+        rid, pid = topo.addr(d, core)
+        m = topo.mask(core, d)
+        g.remote_dma(out_ap=T.land[:, (k - 1) * C + a:(k - 1) * C + b], in_ap=T.xs[:, a:b],
+                     remote_sem=T.sem["a%d_%d" % (region, k)], local_sem=T.sem.sent,
+                     pid=pid, routing_id=rid, dma_engine_mask=m)
+        total += _count(m)
+    return total
+
+
+def _feed_masks(core, helpers, topo):
+    bits = _bits(topo.mask(core, helpers[0]))
+    per = 1
+    while per * 2 * len(helpers) <= len(bits):
+        per *= 2
+    return [sum(1 << e for e in bits[j * per:(j + 1) * per]) for j in range(len(helpers))]
+
+
+def _helper_program(g, core, T, topo, rc, j, helpers):
+    a, b = _block(j)
+    g.wait_ge(T.sem.fed, _count(_feed_masks(rc, helpers, topo)[j]))
+    total = _send_round(g, core, T.rank_of(rc), T, topo, a, b, 1)
+    g.wait_ge(T.sem.sent, total)
+
+
+def _rank_program(g, core, T, topo, rank):
+    S = T.sem
+    v = g.vector
+    helpers = _helpers(core, T, topo)
+    if NH:
+        g.sync.dma_start(T.xs[:, CD:C], T.x[:, CD:C]).then_inc(S.ld1, 16)
+    g.scalar.dma_start(T.xs[:, 0:CD], T.x[:, 0:CD]).then_inc(S.ld0, 16)
+    sent = 0
+    if NH:
+        g.wait_ge(S.ld1, 16)
+        trs = []
+        for j, (h, m) in enumerate(zip(helpers, _feed_masks(core, helpers, topo))):
+            rid, pid = topo.addr(h, core)
+            a, b = _block(j)
+            trs.append(RemoteDMATransfer(dst_ids=[DstId(rid=rid, pnc=pid)], dma_engine_mask=m, remote_sem=S.fed,
+                                         src=T.xs[:, a:b], dst=T.xs[:, a:b]))
+            sent += _count(m)
+        g.remote_dma_fused(trs, local_sem=S.sent)
+    g.wait_ge(S.ld0, 16)
+    sent += _send_round(g, core, rank, T, topo, 0, CD, 0)
+    n = [0]
+
+    def run(ins):
+        ins.then_inc(S.vs, 1)
+        n[0] += 1
+
+    def barrier():
+        v.wait_ge(S.vs, n[0])
+
+    run(v.memset(T.acc[:], 0.0))
+    v.wait_ge(S.ld0, 16)
+    if NH:
+        v.wait_ge(S.ld1, 16)
+    run(v.tensor_copy(T.xp[:], T.xs[:]))
+    span = [(0, CD), (CD, C)]
+    peer = T.cores[(rank + 1) % N]
+    eng = _count(topo.mask(peer, core))
+    need = [eng, eng * NH]
+    stores = []
+    for region, k in ORDER:
+        a, b = span[region]
+        v.wait_ge(S["a%d_%d" % (region, k)], need[region])
+        parts = LAST_SPLIT if k == N - 1 else 1
+        w = (b - a) // parts
+        for p in range(parts):
+            lo, hi = a + p * w, (b if p == parts - 1 else a + (p + 1) * w)
+            src = T.xp if k == 1 else T.q
+            barrier()
+            run(v.tensor_tensor(T.t[:, lo:hi], src[:, lo:hi], T.land[:, (k - 1) * C + lo:(k - 1) * C + hi], AluOpType.subtract))
+            barrier()
+            run(v.tensor_tensor(T.acc[:, lo:hi], T.t[:, lo:hi], T.acc[:, lo:hi], AluOpType.max))
+            if k < N - 1:
+                barrier()
+                run(v.tensor_tensor(T.q[:, lo:hi], T.xp[:, lo:hi], T.acc[:, lo:hi], AluOpType.add))
+            else:
+                stores.append((lo, hi, n[0]))
+    for i, (lo, hi, cnt) in enumerate(stores):
+        qd = g.sync if i % 2 == 0 else g.scalar
+        qd.wait_ge(S.vs, cnt)
+        qd.dma_start(T.y[:, lo:hi], T.acc[:, lo:hi]).then_inc(S["st%d" % i], 16)
+        qd.wait_ge(S["st%d" % i], 16)
+    g.wait_ge(S.sent, sent)
+
+
+def rank_program(g, core, T, topo):
+    rank = T.rank_of(core)
+    if rank is not None:
+        _rank_program(g, core, T, topo, rank)
+        return
+    if NH:
+        for rc in T.cores:
+            hs = _helpers(rc, T, topo)
+            if core in hs:
+                _helper_program(g, core, T, topo, rc, hs.index(core), hs)

@@ -4,23 +4,21 @@ from concourse.mybir import AluOpType
 N = 5
 C = 512
 WORLD = 256
-NH = 0
+NH = 2
 NH_OWN = 0
-CH = 0
+CH = 80
 CD = C - NH * CH
-ORDER = [(0, 1), (0, 2), (0, 3), (0, 4)] if NH == 0 else [(0, 1), (0, 2), (0, 3), (1, 1), (1, 2), (1, 3), (0, 4), (1, 4)]
-LAST_SPLIT = 2 if NH == 0 else 1
+ORDER = [(0, 1), (0, 2), (0, 3), (1, 1), (1, 2), (1, 3), (0, 4), (1, 4)]
 
 SCRATCH = {
     "xs": ("sbuf", [128, C], "float32"),
     "land": ("sbuf", [128, (N - 1) * C], "float32"),
-    "acc": ("sbuf", [128, C], "float32"),
+    "yb": ("sbuf", [128, C], "float32"),
     "xp": ("psum", [128, C], "float32"),
-    "q": ("psum", [128, C], "float32"),
-    "t": ("psum", [128, C], "float32"),
+    "acc": ("psum", [128, C], "float32"),
 }
-SEMAPHORES = (["ld0", "ld1", "fed", "sent", "vs"] + ["a0_%d" % k for k in range(1, N)] + ["a1_%d" % k for k in range(1, N)]
-              + ["st%d" % i for i in range(4)])
+SEMAPHORES = (["ld0", "ld1", "fed", "sent", "vs", "fin0", "fin1", "st0", "st1"]
+              + ["a0_%d" % k for k in range(1, N)] + ["a1_%d" % k for k in range(1, N)])
 
 
 def _bits(mask):
@@ -77,20 +75,18 @@ def _rank_program(g, core, T, topo, rank):
     S = T.sem
     v = g.vector
     helpers = _helpers(core, T, topo)
-    if NH:
-        g.sync.dma_start(T.xs[:, CD:C], T.x[:, CD:C]).then_inc(S.ld1, 16)
+    g.sync.dma_start(T.xs[:, CD:C], T.x[:, CD:C]).then_inc(S.ld1, 16)
     g.scalar.dma_start(T.xs[:, 0:CD], T.x[:, 0:CD]).then_inc(S.ld0, 16)
     sent = 0
-    if NH:
-        g.wait_ge(S.ld1, 16)
-        trs = []
-        for j, (h, m) in enumerate(zip(helpers, _feed_masks(core, helpers, topo))):
-            rid, pid = topo.addr(h, core)
-            a, b = _block(j)
-            trs.append(RemoteDMATransfer(dst_ids=[DstId(rid=rid, pnc=pid)], dma_engine_mask=m, remote_sem=S.fed,
-                                         src=T.xs[:, a:b], dst=T.xs[:, a:b]))
-            sent += _count(m)
-        g.remote_dma_fused(trs, local_sem=S.sent)
+    g.wait_ge(S.ld1, 16)
+    trs = []
+    for j, (h, m) in enumerate(zip(helpers, _feed_masks(core, helpers, topo))):
+        rid, pid = topo.addr(h, core)
+        a, b = _block(j)
+        trs.append(RemoteDMATransfer(dst_ids=[DstId(rid=rid, pnc=pid)], dma_engine_mask=m, remote_sem=S.fed,
+                                     src=T.xs[:, a:b], dst=T.xs[:, a:b]))
+        sent += _count(m)
+    g.remote_dma_fused(trs, local_sem=S.sent)
     g.wait_ge(S.ld0, 16)
     sent += _send_round(g, core, rank, T, topo, 0, CD, 0)
     n = [0]
@@ -102,37 +98,31 @@ def _rank_program(g, core, T, topo, rank):
     def barrier():
         v.wait_ge(S.vs, n[0])
 
-    run(v.memset(T.acc[:], 0.0))
+    run(v.memset(T.yb[:], 4.0))
     v.wait_ge(S.ld0, 16)
-    if NH:
-        v.wait_ge(S.ld1, 16)
+    v.wait_ge(S.ld1, 16)
     run(v.tensor_copy(T.xp[:], T.xs[:]))
+    barrier()
+    run(v.tensor_tensor(T.acc[:], T.xp[:], T.yb[:], AluOpType.mult))
     span = [(0, CD), (CD, C)]
-    peer = T.cores[(rank + 1) % N]
-    eng = _count(topo.mask(peer, core))
+    eng = _count(topo.mask(T.cores[(rank + 1) % N], core))
     need = [eng, eng * NH]
     stores = []
     for region, k in ORDER:
-        a, b = span[region]
+        lo, hi = span[region]
+        slot = T.land[:, (k - 1) * C + lo:(k - 1) * C + hi]
         v.wait_ge(S["a%d_%d" % (region, k)], need[region])
-        parts = LAST_SPLIT if k == N - 1 else 1
-        w = (b - a) // parts
-        for p in range(parts):
-            lo, hi = a + p * w, (b if p == parts - 1 else a + (p + 1) * w)
-            src = T.xp if k == 1 else T.q
-            barrier()
-            run(v.tensor_tensor(T.t[:, lo:hi], src[:, lo:hi], T.land[:, (k - 1) * C + lo:(k - 1) * C + hi], AluOpType.subtract))
-            barrier()
-            run(v.tensor_tensor(T.acc[:, lo:hi], T.t[:, lo:hi], T.acc[:, lo:hi], AluOpType.max))
-            if k < N - 1:
-                barrier()
-                run(v.tensor_tensor(T.q[:, lo:hi], T.xp[:, lo:hi], T.acc[:, lo:hi], AluOpType.add))
-            else:
-                stores.append((lo, hi, n[0]))
-    for i, (lo, hi, cnt) in enumerate(stores):
+        run(v.tensor_tensor(slot, T.xp[:, lo:hi], slot, AluOpType.min))
+        barrier()
+        if k < N - 1:
+            run(v.tensor_tensor(T.acc[:, lo:hi], T.acc[:, lo:hi], slot, AluOpType.subtract))
+        else:
+            v.tensor_tensor(T.yb[:, lo:hi], T.acc[:, lo:hi], slot, AluOpType.subtract).then_inc(S["fin%d" % region], 1)
+            stores.append((lo, hi, region))
+    for i, (lo, hi, region) in enumerate(stores):
         qd = g.sync if i % 2 == 0 else g.scalar
-        qd.wait_ge(S.vs, cnt)
-        qd.dma_start(T.y[:, lo:hi], T.acc[:, lo:hi]).then_inc(S["st%d" % i], 16)
+        qd.wait_ge(S["fin%d" % region], 1)
+        qd.dma_start(T.y[:, lo:hi], T.yb[:, lo:hi]).then_inc(S["st%d" % i], 16)
         qd.wait_ge(S["st%d" % i], 16)
     g.wait_ge(S.sent, sent)
 
@@ -142,8 +132,7 @@ def rank_program(g, core, T, topo):
     if rank is not None:
         _rank_program(g, core, T, topo, rank)
         return
-    if NH:
-        for rc in T.cores:
-            hs = _helpers(rc, T, topo)
-            if core in hs:
-                _helper_program(g, core, T, topo, rc, hs.index(core), hs)
+    for rc in T.cores:
+        hs = _helpers(rc, T, topo)
+        if core in hs:
+            _helper_program(g, core, T, topo, rc, hs.index(core), hs)

@@ -1,138 +1,208 @@
-from concourse.bass import DstId, RemoteDMATransfer
-from concourse.mybir import AluOpType
+from concourse.mybir import AluOpType, ActivationFunctionType
 
 N = 5
 C = 512
-WORLD = 256
-NH = 2
-NH_OWN = 0
-CH = 80
-CD = C - NH * CH
-ORDER = [(0, 1), (0, 2), (0, 3), (1, 1), (1, 2), (1, 3), (0, 4), (1, 4)]
+WID = [104, 104, 104, 100, 100]
+OFF = [0, 104, 208, 312, 412]
+WM = 104
+NR = [26, 26, 26, 25, 25]
+R0 = [0, 26, 52, 78, 103]
 
 SCRATCH = {
     "xs": ("sbuf", [128, C], "float32"),
-    "land": ("sbuf", [128, (N - 1) * C], "float32"),
-    "yb": ("sbuf", [128, C], "float32"),
-    "xp": ("psum", [128, C], "float32"),
-    "acc": ("psum", [128, C], "float32"),
+    "land": ("sbuf", [128, 4 * WM], "float32"),
+    "d": ("sbuf", [128, 10 * WM], "float32"),
+    "p": ("sbuf", [128, 10 * WM], "float32"),
+    "n": ("sbuf", [128, 10 * WM], "float32"),
+    "r1": ("sbuf", [128, 2 * WM], "float32"),
+    "yo": ("sbuf", [128, 5 * WM], "float32"),
+    "yd0": ("dram", [128, WID[0]], "float32"),
+    "yd1": ("dram", [128, WID[1]], "float32"),
+    "yd2": ("dram", [128, WID[2]], "float32"),
+    "yd3": ("dram", [128, WID[3]], "float32"),
+    "yd4": ("dram", [128, WID[4]], "float32"),
+    "xp": ("psum", [128, 4 * WM], "float32"),
+    "ya": ("psum", [128, 4 * WM], "float32"),
+    "y4": ("psum", [128, WM], "float32"),
 }
-SEMAPHORES = (["ld0", "ld1", "fed", "sent", "vs", "fin0", "fin1", "st0", "st1"]
-              + ["a0_%d" % k for k in range(1, N)] + ["a1_%d" % k for k in range(1, N)])
-
-
-def _bits(mask):
-    return [b for b in range(32) if (mask >> b) & 1]
+SEMAPHORES = (["sent", "sty", "stz",
+               "c0", "c1", "c2", "c3", "d1", "d2", "d3", "d40", "d41", "d42", "d43",
+               "r1", "r2p", "r2n", "r3p", "r3n", "r40", "r41", "r42", "r43", "rn0", "rn12", "rn3",
+               "y2", "y30", "y31", "y32", "y3b", "y3c", "s4a", "s4b", "f0", "f1", "f2", "f3", "f4"]
+              + ["l%d" % k for k in range(N)]
+              + ["a%d" % k for k in range(1, N)] + ["b%d" % k for k in range(1, N)])
 
 
 def _count(mask):
-    return len(_bits(mask))
+    return sum((mask >> b) & 1 for b in range(32))
 
 
-def _helpers(rc, T, topo):
-    peers = [d for d in T.cores if d != rc]
-    cand = [c for c in range(WORLD)
-            if topo.host(c) == topo.host(rc) and topo.chip(c) == topo.chip(rc) and T.rank_of(c) is None
-            and all(topo.may_write(c, d) for d in peers)]
-    own = [c for c in cand if topo.die(c) == topo.die(rc)]
-    far = [c for c in cand if topo.die(c) != topo.die(rc)]
-    return far[:NH - NH_OWN] + own[:NH_OWN]
+def _write(g, core, T, topo, dst, out_ap, in_ap, sem):
+    rid, pid = topo.addr(dst, core)
+    m = topo.mask(core, dst)
+    g.remote_dma(out_ap=out_ap, in_ap=in_ap, remote_sem=sem, local_sem=T.sem.sent,
+                 pid=pid, routing_id=rid, dma_engine_mask=m)
+    return _count(m)
 
 
-def _block(j):
-    return CD + j * CH, CD + (j + 1) * CH
-
-
-def _send_round(g, core, rank, T, topo, a, b, region):
-    total = 0
-    for k in range(1, N):
-        d = T.cores[(rank + k) % N]
-        rid, pid = topo.addr(d, core)
-        m = topo.mask(core, d)
-        g.remote_dma(out_ap=T.land[:, (k - 1) * C + a:(k - 1) * C + b], in_ap=T.xs[:, a:b],
-                     remote_sem=T.sem["a%d_%d" % (region, k)], local_sem=T.sem.sent,
-                     pid=pid, routing_id=rid, dma_engine_mask=m)
-        total += _count(m)
-    return total
-
-
-def _feed_masks(core, helpers, topo):
-    bits = _bits(topo.mask(core, helpers[0]))
-    per = 1
-    while per * 2 * len(helpers) <= len(bits):
-        per *= 2
-    return [sum(1 << e for e in bits[j * per:(j + 1) * per]) for j in range(len(helpers))]
-
-
-def _helper_program(g, core, T, topo, rc, j, helpers):
-    a, b = _block(j)
-    g.wait_ge(T.sem.fed, _count(_feed_masks(rc, helpers, topo)[j]))
-    total = _send_round(g, core, T.rank_of(rc), T, topo, a, b, 1)
-    g.wait_ge(T.sem.sent, total)
-
-
-def _rank_program(g, core, T, topo, rank):
+def _rank_program(g, core, T, topo, j):
     S = T.sem
     v = g.vector
-    helpers = _helpers(core, T, topo)
-    g.sync.dma_start(T.xs[:, CD:C], T.x[:, CD:C]).then_inc(S.ld1, 16)
-    g.scalar.dma_start(T.xs[:, 0:CD], T.x[:, 0:CD]).then_inc(S.ld0, 16)
+    sc = g.scalar
+    sy = g.sync
+    add, sub = AluOpType.add, AluOpType.subtract
+    relu = ActivationFunctionType.Relu
+    w = WID[j]
+    o = OFF[j]
+
+    def blk(q):
+        return slice(OFF[q], OFF[q] + WID[q])
+
+    def rows(q):
+        return slice(R0[q], R0[q] + NR[q])
+
+    def cols(a, b):
+        return slice(a * w, b * w)
+
+    def base(k):
+        return k * (k - 1) // 2
+
+    def came(k, back):
+        src = T.cores[(j + k) % N] if back else T.cores[(j - k) % N]
+        return _count(topo.mask(src, core))
+
+    for k in (1, 2, 3, 4, 0):
+        q = (j + k) % N
+        qd = sy if k % 2 == 1 else sc
+        qd.dma_start(T.xs[:, blk(q)], T.x[rows(q), :]).then_inc(S["l%d" % k], 16)
+
     sent = 0
-    g.wait_ge(S.ld1, 16)
-    trs = []
-    for j, (h, m) in enumerate(zip(helpers, _feed_masks(core, helpers, topo))):
-        rid, pid = topo.addr(h, core)
-        a, b = _block(j)
-        trs.append(RemoteDMATransfer(dst_ids=[DstId(rid=rid, pnc=pid)], dma_engine_mask=m, remote_sem=S.fed,
-                                     src=T.xs[:, a:b], dst=T.xs[:, a:b]))
-        sent += _count(m)
-    g.remote_dma_fused(trs, local_sem=S.sent)
-    g.wait_ge(S.ld0, 16)
-    sent += _send_round(g, core, rank, T, topo, 0, CD, 0)
-    n = [0]
-
-    def run(ins):
-        ins.then_inc(S.vs, 1)
-        n[0] += 1
-
-    def barrier():
-        v.wait_ge(S.vs, n[0])
-
-    run(v.memset(T.yb[:], 4.0))
-    v.wait_ge(S.ld0, 16)
-    v.wait_ge(S.ld1, 16)
-    run(v.tensor_copy(T.xp[:], T.xs[:]))
-    barrier()
-    run(v.tensor_tensor(T.acc[:], T.xp[:], T.yb[:], AluOpType.mult))
-    span = [(0, CD), (CD, C)]
-    eng = _count(topo.mask(T.cores[(rank + 1) % N], core))
-    need = [eng, eng * NH]
-    stores = []
-    for region, k in ORDER:
-        lo, hi = span[region]
-        slot = T.land[:, (k - 1) * C + lo:(k - 1) * C + hi]
-        v.wait_ge(S["a%d_%d" % (region, k)], need[region])
-        run(v.tensor_tensor(slot, T.xp[:, lo:hi], slot, AluOpType.min))
-        barrier()
-        if k < N - 1:
-            run(v.tensor_tensor(T.acc[:, lo:hi], T.acc[:, lo:hi], slot, AluOpType.subtract))
-        else:
-            v.tensor_tensor(T.yb[:, lo:hi], T.acc[:, lo:hi], slot, AluOpType.subtract).then_inc(S["fin%d" % region], 1)
-            stores.append((lo, hi, region))
-    for i, (lo, hi, region) in enumerate(stores):
-        qd = g.sync if i % 2 == 0 else g.scalar
-        qd.wait_ge(S["fin%d" % region], 1)
-        qd.dma_start(T.y[:, lo:hi], T.yb[:, lo:hi]).then_inc(S["st%d" % i], 16)
-        qd.wait_ge(S["st%d" % i], 16)
+    for k in range(1, N):
+        q = (j + k) % N
+        wq = WID[q]
+        g.wait_ge(S["l%d" % k], 16)
+        sent += _write(g, core, T, topo, T.cores[q], T.land[:, (k - 1) * wq:k * wq], T.xs[:, blk(q)], S["a%d" % k])
+    place = {1: 2, 2: 1, 3: 0, 4: 4}
+    for m in range(1, N):
+        g.wait_ge(S["f%d" % m], 1)
+        q = (j - m) % N
+        sent += _write(g, core, T, topo, T.cores[q], T["yd%d" % j][:], T.yo[:, cols(place[m], place[m] + 1)],
+                       S["b%d" % m])
     g.wait_ge(S.sent, sent)
+
+    def slot(k):
+        return T.land[:, cols(k - 1, k)]
+
+    def grp(buf, k, a, b):
+        return buf[:, cols(base(k) + a, base(k) + b)]
+
+    def diff(k, i, sem):
+        s = k - 1 - i
+        v.tensor_tensor(grp(T.d, k, i, i + 1), T.xp[:, cols(s, s + 1)], slot(k), sub).then_inc(sem, 1)
+
+    def ya(a, b):
+        return T.ya[:, cols(a, b)]
+
+    v.wait_ge(S.l0, 16)
+    v.tensor_copy(T.xp[:, cols(0, 1)], T.xs[:, o:o + w]).then_inc(S.c0, 1)
+    v.wait_ge(S.a1, came(1, False))
+    v.wait_ge(S.c0, 1)
+    diff(1, 0, S.d1)
+    v.tensor_copy(T.xp[:, cols(1, 2)], slot(1)).then_inc(S.c1, 1)
+    v.wait_ge(S.a2, came(2, False))
+    v.wait_ge(S.c1, 1)
+    diff(2, 0, S.d2)
+    diff(2, 1, S.d2)
+    v.tensor_copy(T.xp[:, cols(2, 3)], slot(2)).then_inc(S.c2, 1)
+    v.wait_ge(S.r1, 2)
+    v.wait_ge(S.r2p, 1)
+    v.tensor_tensor(ya(2, 4), T.r1[:, cols(0, 2)], grp(T.p, 2, 0, 2), add).then_inc(S.y2, 1)
+    v.wait_ge(S.r2n, 1)
+    v.tensor_tensor(ya(1, 2), grp(T.n, 2, 0, 1), grp(T.n, 2, 1, 2), add).then_inc(S.y2, 1)
+    v.wait_ge(S.a3, came(3, False))
+    v.wait_ge(S.c2, 1)
+    for i in range(3):
+        diff(3, i, S.d3)
+    v.tensor_copy(T.xp[:, cols(3, 4)], slot(3)).then_inc(S.c3, 1)
+    v.wait_ge(S.a4, came(4, False))
+    diff(4, 2, S.d41)
+    v.wait_ge(S.r3p, 1)
+    v.wait_ge(S.y2, 2)
+    v.tensor_tensor(ya(2, 3), ya(2, 3), grp(T.p, 3, 1, 2), add).then_inc(S.y31, 1)
+    diff(4, 1, S.d42)
+    v.wait_ge(S.r41, 1)
+    v.wait_ge(S.y31, 1)
+    v.tensor_tensor(T.yo[:, cols(2, 3)], ya(2, 3), grp(T.p, 4, 2, 3), add).then_inc(S.f1, 1)
+    v.tensor_tensor(ya(1, 2), ya(1, 2), grp(T.p, 3, 0, 1), add).then_inc(S.y32, 1)
+    v.wait_ge(S.c3, 1)
+    diff(4, 0, S.d43)
+    v.wait_ge(S.r42, 1)
+    v.wait_ge(S.y32, 1)
+    v.tensor_tensor(T.yo[:, cols(1, 2)], ya(1, 2), grp(T.p, 4, 1, 2), add).then_inc(S.f2, 1)
+    diff(4, 3, S.d40)
+    v.wait_ge(S.r3n, 1)
+    v.tensor_tensor(ya(0, 1), grp(T.n, 3, 0, 1), grp(T.n, 3, 1, 2), add).then_inc(S.y3b, 1)
+    v.wait_ge(S.rn12, 1)
+    v.tensor_tensor(T.y4[:, 0:w], grp(T.n, 4, 1, 2), grp(T.n, 4, 2, 3), add).then_inc(S.s4a, 1)
+    v.wait_ge(S.y3b, 1)
+    v.tensor_tensor(ya(0, 1), ya(0, 1), grp(T.n, 3, 2, 3), add).then_inc(S.y3c, 1)
+    v.wait_ge(S.rn3, 1)
+    v.wait_ge(S.s4a, 1)
+    v.tensor_tensor(T.y4[:, 0:w], T.y4[:, 0:w], grp(T.n, 4, 0, 1), add).then_inc(S.s4b, 1)
+    v.wait_ge(S.r43, 1)
+    v.wait_ge(S.y3c, 1)
+    v.tensor_tensor(T.yo[:, cols(0, 1)], ya(0, 1), grp(T.p, 4, 0, 1), add).then_inc(S.f3, 1)
+    v.wait_ge(S.rn0, 1)
+    v.wait_ge(S.s4b, 1)
+    v.tensor_tensor(T.yo[:, cols(4, 5)], T.y4[:, 0:w], grp(T.n, 4, 3, 4), add).then_inc(S.f4, 1)
+    v.tensor_tensor(ya(3, 4), ya(3, 4), grp(T.p, 3, 2, 3), add).then_inc(S.y30, 1)
+    v.wait_ge(S.r40, 1)
+    v.wait_ge(S.y30, 1)
+    v.tensor_tensor(T.yo[:, cols(3, 4)], ya(3, 4), grp(T.p, 4, 3, 4), add).then_inc(S.f0, 1)
+
+    def act(out, in_, sem, neg=False):
+        if neg:
+            sc.activation(out, in_, relu, scale=-1.0).then_inc(sem, 1)
+        else:
+            sc.activation(out, in_, relu).then_inc(sem, 1)
+
+    sc.wait_ge(S.d1, 1)
+    act(T.r1[:, cols(0, 1)], grp(T.d, 1, 0, 1), S.r1, neg=True)
+    act(T.r1[:, cols(1, 2)], grp(T.d, 1, 0, 1), S.r1)
+    sc.wait_ge(S.d2, 2)
+    act(grp(T.p, 2, 0, 2), grp(T.d, 2, 0, 2), S.r2p)
+    act(grp(T.n, 2, 0, 2), grp(T.d, 2, 0, 2), S.r2n, neg=True)
+    sc.wait_ge(S.d3, 3)
+    act(grp(T.p, 3, 0, 3), grp(T.d, 3, 0, 3), S.r3p)
+    sc.wait_ge(S.d41, 1)
+    act(grp(T.p, 4, 2, 3), grp(T.d, 4, 2, 3), S.r41)
+    sc.wait_ge(S.d42, 1)
+    act(grp(T.p, 4, 1, 2), grp(T.d, 4, 1, 2), S.r42)
+    act(grp(T.n, 3, 0, 3), grp(T.d, 3, 0, 3), S.r3n, neg=True)
+    act(grp(T.n, 4, 1, 3), grp(T.d, 4, 1, 3), S.rn12, neg=True)
+    sc.wait_ge(S.d43, 1)
+    act(grp(T.p, 4, 0, 1), grp(T.d, 4, 0, 1), S.r43)
+    act(grp(T.n, 4, 0, 1), grp(T.d, 4, 0, 1), S.rn3, neg=True)
+    sc.wait_ge(S.d40, 1)
+    act(grp(T.n, 4, 3, 4), grp(T.d, 4, 3, 4), S.rn0, neg=True)
+    act(grp(T.p, 4, 3, 4), grp(T.d, 4, 3, 4), S.r40)
+
+    def store_back(qd, m, sem):
+        own = (j + m) % N
+        qd.wait_ge(S["b%d" % m], came(m, True))
+        qd.dma_start(T.y[rows(own), :], T["yd%d" % own][:]).then_inc(sem, 16)
+
+    store_back(sy, 1, S.sty)
+    sy.wait_ge(S.f0, 1)
+    sy.dma_start(T.y[rows(j), :], T.yo[:, cols(3, 4)]).then_inc(S.sty, 16)
+    store_back(sy, 3, S.sty)
+    sy.wait_ge(S.sty, 48)
+    store_back(sc, 2, S.stz)
+    store_back(sc, 4, S.stz)
+    sc.wait_ge(S.stz, 32)
 
 
 def rank_program(g, core, T, topo):
     rank = T.rank_of(core)
     if rank is not None:
         _rank_program(g, core, T, topo, rank)
-        return
-    for rc in T.cores:
-        hs = _helpers(rc, T, topo)
-        if core in hs:
-            _helper_program(g, core, T, topo, rc, hs.index(core), hs)

from concourse.mybir import AluOpType, ActivationFunctionType

N = 5
C = 512
WID = [104, 104, 104, 100, 100]
OFF = [0, 104, 208, 312, 412]
WM = 104
NR = [26, 26, 26, 25, 25]
R0 = [0, 26, 52, 78, 103]

SCRATCH = {
    "xs": ("sbuf", [128, C], "float32"),
    "land": ("sbuf", [128, 4 * WM], "float32"),
    "d": ("sbuf", [128, 10 * WM], "float32"),
    "p": ("sbuf", [128, 10 * WM], "float32"),
    "n": ("sbuf", [128, 10 * WM], "float32"),
    "r1": ("sbuf", [128, 2 * WM], "float32"),
    "yo": ("sbuf", [128, 5 * WM], "float32"),
    "yd0": ("dram", [128, WID[0]], "float32"),
    "yd1": ("dram", [128, WID[1]], "float32"),
    "yd2": ("dram", [128, WID[2]], "float32"),
    "yd3": ("dram", [128, WID[3]], "float32"),
    "yd4": ("dram", [128, WID[4]], "float32"),
    "xp": ("psum", [128, 4 * WM], "float32"),
    "ya": ("psum", [128, 4 * WM], "float32"),
    "y4": ("psum", [128, WM], "float32"),
}
SEMAPHORES = (["sent", "sty", "stz",
               "c0", "c1", "c2", "c3", "d1", "d2", "d3", "d40", "d41", "d42", "d43",
               "r1", "r2p", "r2n", "r3p", "r3n", "r40", "r41", "r42", "r43", "rn0", "rn12", "rn3",
               "y2", "y30", "y31", "y32", "y3b", "y3c", "s4a", "s4b", "f0", "f1", "f2", "f3", "f4"]
              + ["l%d" % k for k in range(N)]
              + ["a%d" % k for k in range(1, N)] + ["b%d" % k for k in range(1, N)])


def _count(mask):
    return sum((mask >> b) & 1 for b in range(32))


def _write(g, core, T, topo, dst, out_ap, in_ap, sem):
    rid, pid = topo.addr(dst, core)
    m = topo.mask(core, dst)
    g.remote_dma(out_ap=out_ap, in_ap=in_ap, remote_sem=sem, local_sem=T.sem.sent,
                 pid=pid, routing_id=rid, dma_engine_mask=m)
    return _count(m)


def _rank_program(g, core, T, topo, j):
    S = T.sem
    v = g.vector
    sc = g.scalar
    sy = g.sync
    add, sub = AluOpType.add, AluOpType.subtract
    relu = ActivationFunctionType.Relu
    w = WID[j]
    o = OFF[j]

    def blk(q):
        return slice(OFF[q], OFF[q] + WID[q])

    def rows(q):
        return slice(R0[q], R0[q] + NR[q])

    def cols(a, b):
        return slice(a * w, b * w)

    def base(k):
        return k * (k - 1) // 2

    def came(k, back):
        src = T.cores[(j + k) % N] if back else T.cores[(j - k) % N]
        return _count(topo.mask(src, core))

    for k in (1, 2, 3, 4, 0):
        q = (j + k) % N
        qd = sy if k % 2 == 1 else sc
        qd.dma_start(T.xs[:, blk(q)], T.x[rows(q), :]).then_inc(S["l%d" % k], 16)

    sent = 0
    for k in range(1, N):
        q = (j + k) % N
        wq = WID[q]
        g.wait_ge(S["l%d" % k], 16)
        sent += _write(g, core, T, topo, T.cores[q], T.land[:, (k - 1) * wq:k * wq], T.xs[:, blk(q)], S["a%d" % k])
    place = {1: 2, 2: 1, 3: 0, 4: 4}
    for m in range(1, N):
        g.wait_ge(S["f%d" % m], 1)
        q = (j - m) % N
        sent += _write(g, core, T, topo, T.cores[q], T["yd%d" % j][:], T.yo[:, cols(place[m], place[m] + 1)],
                       S["b%d" % m])
    g.wait_ge(S.sent, sent)

    def slot(k):
        return T.land[:, cols(k - 1, k)]

    def grp(buf, k, a, b):
        return buf[:, cols(base(k) + a, base(k) + b)]

    def diff(k, i, sem):
        s = k - 1 - i
        v.tensor_tensor(grp(T.d, k, i, i + 1), T.xp[:, cols(s, s + 1)], slot(k), sub).then_inc(sem, 1)

    def ya(a, b):
        return T.ya[:, cols(a, b)]

    v.wait_ge(S.l0, 16)
    v.tensor_copy(T.xp[:, cols(0, 1)], T.xs[:, o:o + w]).then_inc(S.c0, 1)
    v.wait_ge(S.a1, came(1, False))
    v.wait_ge(S.c0, 1)
    diff(1, 0, S.d1)
    v.tensor_copy(T.xp[:, cols(1, 2)], slot(1)).then_inc(S.c1, 1)
    v.wait_ge(S.a2, came(2, False))
    v.wait_ge(S.c1, 1)
    diff(2, 0, S.d2)
    diff(2, 1, S.d2)
    v.tensor_copy(T.xp[:, cols(2, 3)], slot(2)).then_inc(S.c2, 1)
    v.wait_ge(S.r1, 2)
    v.wait_ge(S.r2p, 1)
    v.tensor_tensor(ya(2, 4), T.r1[:, cols(0, 2)], grp(T.p, 2, 0, 2), add).then_inc(S.y2, 1)
    v.wait_ge(S.r2n, 1)
    v.tensor_tensor(ya(1, 2), grp(T.n, 2, 0, 1), grp(T.n, 2, 1, 2), add).then_inc(S.y2, 1)
    v.wait_ge(S.a3, came(3, False))
    v.wait_ge(S.c2, 1)
    for i in range(3):
        diff(3, i, S.d3)
    v.tensor_copy(T.xp[:, cols(3, 4)], slot(3)).then_inc(S.c3, 1)
    v.wait_ge(S.a4, came(4, False))
    diff(4, 2, S.d41)
    v.wait_ge(S.r3p, 1)
    v.wait_ge(S.y2, 2)
    v.tensor_tensor(ya(2, 3), ya(2, 3), grp(T.p, 3, 1, 2), add).then_inc(S.y31, 1)
    diff(4, 1, S.d42)
    v.wait_ge(S.r41, 1)
    v.wait_ge(S.y31, 1)
    v.tensor_tensor(T.yo[:, cols(2, 3)], ya(2, 3), grp(T.p, 4, 2, 3), add).then_inc(S.f1, 1)
    v.tensor_tensor(ya(1, 2), ya(1, 2), grp(T.p, 3, 0, 1), add).then_inc(S.y32, 1)
    v.wait_ge(S.c3, 1)
    diff(4, 0, S.d43)
    v.wait_ge(S.r42, 1)
    v.wait_ge(S.y32, 1)
    v.tensor_tensor(T.yo[:, cols(1, 2)], ya(1, 2), grp(T.p, 4, 1, 2), add).then_inc(S.f2, 1)
    diff(4, 3, S.d40)
    v.wait_ge(S.r3n, 1)
    v.tensor_tensor(ya(0, 1), grp(T.n, 3, 0, 1), grp(T.n, 3, 1, 2), add).then_inc(S.y3b, 1)
    v.wait_ge(S.rn12, 1)
    v.tensor_tensor(T.y4[:, 0:w], grp(T.n, 4, 1, 2), grp(T.n, 4, 2, 3), add).then_inc(S.s4a, 1)
    v.wait_ge(S.y3b, 1)
    v.tensor_tensor(ya(0, 1), ya(0, 1), grp(T.n, 3, 2, 3), add).then_inc(S.y3c, 1)
    v.wait_ge(S.rn3, 1)
    v.wait_ge(S.s4a, 1)
    v.tensor_tensor(T.y4[:, 0:w], T.y4[:, 0:w], grp(T.n, 4, 0, 1), add).then_inc(S.s4b, 1)
    v.wait_ge(S.r43, 1)
    v.wait_ge(S.y3c, 1)
    v.tensor_tensor(T.yo[:, cols(0, 1)], ya(0, 1), grp(T.p, 4, 0, 1), add).then_inc(S.f3, 1)
    v.wait_ge(S.rn0, 1)
    v.wait_ge(S.s4b, 1)
    v.tensor_tensor(T.yo[:, cols(4, 5)], T.y4[:, 0:w], grp(T.n, 4, 3, 4), add).then_inc(S.f4, 1)
    v.tensor_tensor(ya(3, 4), ya(3, 4), grp(T.p, 3, 2, 3), add).then_inc(S.y30, 1)
    v.wait_ge(S.r40, 1)
    v.wait_ge(S.y30, 1)
    v.tensor_tensor(T.yo[:, cols(3, 4)], ya(3, 4), grp(T.p, 4, 3, 4), add).then_inc(S.f0, 1)

    def act(out, in_, sem, neg=False):
        if neg:
            sc.activation(out, in_, relu, scale=-1.0).then_inc(sem, 1)
        else:
            sc.activation(out, in_, relu).then_inc(sem, 1)

    sc.wait_ge(S.d1, 1)
    act(T.r1[:, cols(0, 1)], grp(T.d, 1, 0, 1), S.r1, neg=True)
    act(T.r1[:, cols(1, 2)], grp(T.d, 1, 0, 1), S.r1)
    sc.wait_ge(S.d2, 2)
    act(grp(T.p, 2, 0, 2), grp(T.d, 2, 0, 2), S.r2p)
    act(grp(T.n, 2, 0, 2), grp(T.d, 2, 0, 2), S.r2n, neg=True)
    sc.wait_ge(S.d3, 3)
    act(grp(T.p, 3, 0, 3), grp(T.d, 3, 0, 3), S.r3p)
    sc.wait_ge(S.d41, 1)
    act(grp(T.p, 4, 2, 3), grp(T.d, 4, 2, 3), S.r41)
    sc.wait_ge(S.d42, 1)
    act(grp(T.p, 4, 1, 2), grp(T.d, 4, 1, 2), S.r42)
    act(grp(T.n, 3, 0, 3), grp(T.d, 3, 0, 3), S.r3n, neg=True)
    act(grp(T.n, 4, 1, 3), grp(T.d, 4, 1, 3), S.rn12, neg=True)
    sc.wait_ge(S.d43, 1)
    act(grp(T.p, 4, 0, 1), grp(T.d, 4, 0, 1), S.r43)
    act(grp(T.n, 4, 0, 1), grp(T.d, 4, 0, 1), S.rn3, neg=True)
    sc.wait_ge(S.d40, 1)
    act(grp(T.n, 4, 3, 4), grp(T.d, 4, 3, 4), S.rn0, neg=True)
    act(grp(T.p, 4, 3, 4), grp(T.d, 4, 3, 4), S.r40)

    def store_back(qd, m, sem):
        own = (j + m) % N
        qd.wait_ge(S["b%d" % m], came(m, True))
        qd.dma_start(T.y[rows(own), :], T["yd%d" % own][:]).then_inc(sem, 16)

    store_back(sy, 1, S.sty)
    sy.wait_ge(S.f0, 1)
    sy.dma_start(T.y[rows(j), :], T.yo[:, cols(3, 4)]).then_inc(S.sty, 16)
    store_back(sy, 3, S.sty)
    sy.wait_ge(S.sty, 48)
    store_back(sc, 2, S.stz)
    store_back(sc, 4, S.stz)
    sc.wait_ge(S.stz, 32)


def rank_program(g, core, T, topo):
    rank = T.rank_of(core)
    if rank is not None:
        _rank_program(g, core, T, topo, rank)
